import numpy as np
import ml_dtypes


def mxq(x, axis, fmt="e4m3"):
    dtype, down = {"e4m3": (ml_dtypes.float8_e4m3fn, 7), "e5m2": (ml_dtypes.float8_e5m2, 14)}[fmt]
    v = np.moveaxis(np.asarray(x, np.float32).astype(ml_dtypes.bfloat16).astype(np.float64), axis, -1)
    blocks = v.reshape(v.shape[:-1] + (-1, 32))
    amax = np.abs(blocks).max(-1, keepdims=True)
    byte = np.maximum(np.where(amax > 0, np.frexp(amax)[1] - 1 + 127, 0) - down, 1)
    scale = np.exp2(byte - 127.0)
    codes = (blocks / scale).astype(np.float32).astype(dtype).astype(np.float64)
    return np.moveaxis((codes * scale).reshape(v.shape), -1, axis)


WIDE = False


def mx_kscale(k):
    if not WIDE:
        return np.ones(k)
    levels = np.array([10, -10, 5, -5, 0])
    if k % 512:
        return np.exp2(np.random.permutation(np.resize(levels, k // 32))).repeat(32)
    a = np.empty((k // 512, 16))
    for p in range(k // 512):
        a[p, :8] = np.random.permutation(np.resize(levels, 8))
        for g in range(8):
            far = levels[np.abs(levels - a[p, g]) >= 10]
            a[p, g + 8] = far[np.random.randint(len(far))]
    return np.exp2(a.ravel()).repeat(32)


def f64(x):
    return np.asarray(x).astype(np.float64)


def striped(idx):
    return np.tile(idx.reshape(-1, 16).T, (8, 1)).astype(np.uint16)


def unstriped(offs):
    return offs[:16].T.reshape(-1).astype(np.int64)


E2M1 = np.array([0.0, 0.5, 1.0, 1.5, 2.0, 3.0, 4.0, 6.0, -0.0, -0.5, -1.0, -1.5, -2.0, -3.0, -4.0, -6.0])


def pack_weight(w, fmt):
    k, n = w.shape
    w = f64(np.asarray(w, np.float32).astype(ml_dtypes.bfloat16)).reshape(k // 32, 32, n)
    amax = np.abs(w).max(1)
    if fmt == "e4m3":
        byte = np.frexp(amax)[1] - 1 + 127 - 7
    else:
        mant, ex = np.frexp(amax / 6.0)
        byte = np.where(mant > 0.5, ex, ex - 1) + 127
    byte = np.clip(np.where(amax > 0, byte, 1), 1, 254)
    scaled = (w * np.exp2(127.0 - byte)[:, None, :]).reshape(k, n).astype(np.float32)
    by_word = np.ascontiguousarray(scaled.reshape(k // 512, 128, 4, n).transpose(0, 1, 3, 2))
    if fmt == "e4m3":
        words = by_word.astype(ml_dtypes.float8_e4m3fn).view(np.uint8)
    else:
        c = by_word.astype(ml_dtypes.float4_e2m1fn).view(np.uint8) & 0xF
        words = (c[..., 0::2] | (c[..., 1::2] << 4)).reshape(k // 512, 128, 2 * n)
    return np.ascontiguousarray(words), np.ascontiguousarray(byte.astype(np.uint8).reshape(k // 512, 16, n))


def unpack_weight(words, scales, fmt):
    g, _, n = scales.shape
    words = np.ascontiguousarray(words).reshape(g, 128, n, -1)
    if fmt == "e4m3":
        vals = words.view(ml_dtypes.float8_e4m3fn).astype(np.float64)
    else:
        nib = np.empty((g, 128, n, 4), np.uint8)
        nib[..., 0::2] = words & 0xF
        nib[..., 1::2] = words >> 4
        vals = E2M1[nib]
    vals = vals * np.repeat(np.exp2(scales.astype(np.float64) - 127.0), 8, axis=1)[..., None]
    return vals.transpose(0, 1, 3, 2).reshape(g * 512, n)


def gelu(v):
    return 0.5 * v * (1.0 + np.tanh(np.sqrt(2.0 / np.pi) * (v + 0.044715 * v**3)))


K, H, N, T, S, T2, P = 512, 1024, 384, 4096, 1024, 2048, 512

def setup_inputs():
    n = np.random.standard_normal
    s = mx_kscale(K)[:, None]
    u = mx_kscale(H)[:, None]
    perm = np.random.permutation(T2)
    tab_words, tab_scales = pack_weight(n((K, T)) * s, "e4m3")
    w2_words, w2_scales = pack_weight(1.5 * n((K, H)) / np.sqrt(K) / s, "e2m1")
    return {
        "tab_words": tab_words, "tab_scales": tab_scales,
        "offs": striped(np.random.permutation(T)[:S]),
        "offs2": striped(np.random.permutation(T2)[:S]),
        "offs3": striped(perm[:P]),
        "offs4": striped(perm[P:2 * P]),
        "w1": (2.0 * n((K, H)) / np.sqrt(K) / s * u.T).astype(np.float32),
        "w2_words": w2_words, "w2_scales": w2_scales,
        "wgs": np.exp(0.3 * n((128, S))).astype(np.float32),
        "page0": (n((H, T2)) * u).astype(np.float32),
        "lift": (0.8 * n(H) * u[:, 0]).astype(np.float32),
        "w4": (n((H, N)) / np.sqrt(H) / u).astype(np.float32),
        "gain": np.exp(0.3 * n(N)).astype(np.float32),
    }

def reference(tab_words, tab_scales, offs, offs2, offs3, offs4, w1, w2_words, w2_scales, wgs, page0, lift, w4, gain):
    v = unpack_weight(tab_words, tab_scales, "e4m3")[:, unstriped(offs)]
    w2 = unpack_weight(w2_words, w2_scales, "e2m1")
    bid = mxq(f64(w1), 0, "e4m3").T @ v
    spread = w2.T @ v
    h = bid / (1.0 + np.abs(spread))
    page = f64(page0).copy()
    page[:, unstriped(offs2)] = np.tile(f64(wgs), (H // 128, 1)) * h
    a = page[:, unstriped(offs3)]
    b = page[:, unstriped(offs4)]
    page[:, unstriped(offs3)] = np.maximum(a, b)
    page[:, unstriped(offs4)] = np.minimum(a, b) + f64(lift)[:, None]
    y = mxq(f64(w4), 0, "e4m3").T @ mxq(page, 0, "e4m3")
    return y * f64(gain)[:, None]

@@ -1,0 +1,331 @@
+from contextlib import ExitStack
+
+import concourse.mybir as mybir
+
+K, H, N, T, S, T2, PAIRS = 512, 1024, 384, 4096, 1024, 2048, 512
+FLOPS = 2 * (2 * K * H * S + H * N * T2)
+
+F32 = mybir.dt.float32
+BF16 = mybir.dt.bfloat16
+I32 = mybir.dt.int32
+U32 = mybir.dt.uint32
+U16 = mybir.dt.uint16
+U8 = mybir.dt.uint8
+FP8X4 = mybir.dt.float8_e4m3fn_x4
+FP4X4 = mybir.dt.float4_e2m1fn_x4
+ACT = mybir.ActivationFunctionType
+ALU = mybir.AluOpType
+
+P = 128
+PACK = 4
+BANK = 512
+PASSES = H // (P * PACK)
+CHUNKS = T2 // BANK
+NB = N // P
+SLICES = [(0, 0), (0, 1), (0, 2), (0, 3), (1, 2), (1, 0), (1, 1), (1, 3)]
+BANKS = 8
+
+
+def tile_list_bill_demand_sheet_kernel(
+    tc, tab_words, tab_scales, offs, offs2, offs3, offs4, w1, w2_words, w2_scales, wgs, page0, lift, w4, gain, out
+):
+    nc = tc.nc
+    with ExitStack() as ctx:
+        pool = ctx.enter_context(tc.tile_pool(name="sb", bufs=1))
+        psum = ctx.enter_context(tc.psum_pool(name="ps", bufs=1))
+
+        def sb(shape, dtype, tag, bufs=1):
+            return pool.tile(shape, dtype, name=tag, tag=tag, bufs=bufs, align_bytes=64)
+
+        def bank(i):
+            return psum.tile([P, BANK], F32, name="bank%d" % i, tag="bank%d" % i)
+
+        page_rows = page0.rearrange("(b p t) c -> b t p c", b=PASSES, t=PACK)
+        w1_rows = w1.rearrange("(p j) (b c) -> b p j c", j=PACK, b=PASSES)
+        w4_rows = w4.rearrange("(b p j) n -> b p j n", b=PASSES, j=PACK)
+        wgs_rows = wgs.rearrange("(q t) j -> q t j", t=PACK)
+        out_rows = out.rearrange("(nb p) c -> nb p c", p=P)
+
+        pick = sb([P, S // 16], U16, "pick")
+        nc.sync.dma_start(pick[:], offs)
+        tab_s = sb([P, T], U8, "tab_s")
+        nc.vector.memset(tab_s[:].bitcast(I32), 0)
+        w2s_raw = sb([P, H], U8, "w2s_raw")
+        nc.vector.memset(w2s_raw[:].bitcast(I32), 0)
+        tab_w = sb([P, T], U32, "tab_w")
+        tab_rows = tab_words[0].rearrange("p t i -> p (t i)").bitcast(I32)
+
+        def load_plane(plane, rows, q):
+            nc.sync.dma_start(plane[32 * q : 32 * q + 4, :].bitcast(I32), rows[0, 4 * q : 4 * q + 4, :].bitcast(I32))
+
+        nc.sync.dma_start(tab_w[:, : T // 2].bitcast(I32), tab_rows[:, : T // 2])
+        for q in range(4):
+            load_plane(tab_s, tab_scales, q)
+        w2_raw = sb([P, 2 * H], U8, "w2_raw")
+        nc.sync.dma_start(w2_raw[:].bitcast(I32), w2_words[0].bitcast(I32))
+        load_plane(w2s_raw, w2_scales, 0)
+        nc.sync.dma_start(tab_w[:, T // 2 :].bitcast(I32), tab_rows[:, T // 2 :])
+        for q in range(1, 4):
+            load_plane(w2s_raw, w2_scales, q)
+
+        def load_w1(b):
+            raw = sb([P, PACK, BANK], F32, "raw%d" % b)
+            nc.sync.dma_start(raw[:], w1_rows[b])
+            return raw
+
+        def load_w4(b):
+            raw = sb([P, PACK, N], F32, "raw%d" % b)
+            nc.sync.dma_start(raw[:], w4_rows[b])
+            return raw
+
+        pages = {}
+
+        def load_page(s):
+            b, t = SLICES[s]
+            pages[s] = sb([P, T2], F32, "page", bufs=5)
+            nc.sync.dma_start(pages[s][:], page_rows[b, t])
+
+        w1_raw = {0: load_w1(0)}
+        load_page(0)
+        put = sb([P, S // 16], U16, "put")
+        nc.sync.dma_start(put[:], offs2)
+        wg_first = sb([P, S], F32, "wg_first")
+        for q in range(4):
+            nc.sync.dma_start(wg_first[32 * q : 32 * q + 32, :], wgs_rows[:, 0, :])
+        upper = sb([P, PAIRS // 16], U16, "upper")
+        nc.sync.dma_start(upper[:], offs3)
+        lower = sb([P, PAIRS // 16], U16, "lower")
+        nc.sync.dma_start(lower[:], offs4)
+        lift_t = sb([P, PASSES, PACK], F32, "lift_t")
+        gain_t = sb([P, NB], F32, "gain_t")
+        with nc.allow_non_contiguous_dma(reason="one value a row"):
+            nc.sync.dma_start(lift_t[:], lift.rearrange("(b p t) -> p b t", b=PASSES, t=PACK))
+            nc.sync.dma_start(gain_t[:], gain.rearrange("(nb p) -> p nb", p=P))
+        wg_rest = sb([P, PACK - 1, S], F32, "wg_rest")
+        for q in range(4):
+            nc.sync.dma_start(wg_rest[32 * q : 32 * q + 32, :, :], wgs_rows[:, 1:PACK, :])
+        load_page(1)
+        w1_raw[1] = load_w1(1)
+        load_page(2)
+        load_page(3)
+        load_page(4)
+
+        def wg(t):
+            return wg_first[:] if t == 0 else wg_rest[:, t - 1, :]
+
+        w2_c = sb([P, 2 * H], U8, "w2_c")
+        w2_s = sb([P, H], U8, "w2_s")
+        nc.vector.tensor_copy(
+            w2_c[:].bitcast(U16).rearrange("p (b t m) -> p b t m", b=PASSES, t=PACK),
+            w2_raw[:].bitcast(U16).rearrange("p (b m t) -> p b t m", b=PASSES, t=PACK),
+        )
+
+        def deal_w2_scales(b):
+            cols = slice(b * BANK, (b + 1) * BANK)
+            nc.vector.tensor_copy(
+                w2_s[:, cols].rearrange("p (t m) -> p t m", t=PACK),
+                w2s_raw[:, cols].rearrange("p (m t) -> p t m", t=PACK),
+            )
+
+        v_c = sb([P, S], U32, "v_c")
+        v_s = sb([P, S], U8, "v_s")
+        HALVES = S // BANK
+
+        def half(h):
+            return slice(h * BANK, (h + 1) * BANK)
+
+        def half_list(h):
+            return slice(h * BANK // 16, (h + 1) * BANK // 16)
+
+        for h in range(HALVES):
+            nc.vector.tensor_copy(v_s[:, half(h)], tab_s[:].indirect(pick[:, half_list(h)]))
+        deal_w2_scales(0)
+        for h in range(HALVES):
+            nc.vector.tensor_copy(v_c[:, half(h)], tab_w[:].indirect(pick[:, half_list(h)]))
+
+        w1_c, w1_s, w4_c, w4_s = {}, {}, {}, {}
+
+        def quantise_w1(b, copy):
+            grouped = sb([P, PACK * BANK], BF16, "grouped%d" % b)
+            copy(
+                grouped[:].rearrange("p (t m j) -> p m t j", t=PACK, j=PACK),
+                w1_raw[b][:].rearrange("p j (m t) -> p m t j", t=PACK),
+            )
+            w1_c[b] = sb([P, BANK], U32, "w1_c%d" % b)
+            w1_s[b] = sb([P, BANK], U8, "w1_s%d" % b)
+            nc.vector.quantize_mx(w1_c[b][:].bitcast(FP8X4), w1_s[b][:], grouped[:])
+
+        def quantise_w4(b, raw):
+            grouped = sb([P, PACK * N], BF16, "grouped%d" % b)
+            nc.scalar.copy(grouped[:].rearrange("p (n j) -> p n j", j=PACK), raw[:].rearrange("p j n -> p n j"))
+            w4_c[b] = sb([P, N], U32, "w4_c%d" % b)
+            w4_s[b] = sb([P, N], U8, "w4_s%d" % b)
+            nc.vector.quantize_mx(w4_c[b][:].bitcast(FP8X4), w4_s[b][:], grouped[:])
+
+        damp = {-2: sb([P, S], F32, "pair0"), -1: sb([P, S], F32, "pair1")}
+        SPREAD_BANKS = [0, 1, 4, 5, 6, 7]
+        both_halves = [half(h) for h in range(HALVES)]
+        whole = [slice(0, S)]
+
+        def log_spread(batch, cuts):
+            for s in batch:
+                b, t = SLICES[s]
+                c0 = (b * PACK + t) * P
+                damp[s] = sb([P, S], F32, "damp%d" % s)
+                for h in range(HALVES):
+                    acc = bank(SPREAD_BANKS[(HALVES * s + h) % len(SPREAD_BANKS)])
+                    nc.tensor.matmul_mx(
+                        acc[:], lhsT=w2_c[:, 2 * c0 : 2 * (c0 + P)].bitcast(FP4X4), lhsT_scale=w2_s[:, c0 : c0 + P],
+                        rhs=v_c[:, half(h)].bitcast(FP8X4), rhs_scale=v_s[:, half(h)], start=True, stop=True,
+                    )
+                    nc.scalar.activation(damp[s][:, half(h)], acc[:], ACT.Abs)
+            for s in batch:
+                for c in cuts:
+                    nc.scalar.activation(damp[s][:, c], damp[s][:, c], ACT.Ln, bias=1.0)
+
+        def invert(batch, cuts):
+            for s in batch:
+                for c in cuts:
+                    nc.scalar.activation(damp[s][:, c], damp[s][:, c], ACT.Exp, scale=-1.0)
+
+        hid = {}
+
+        def damped_bid(s, h):
+            b, t = SLICES[s]
+            if h == 0:
+                hid[s] = damp[s - 5] if s >= 3 else (hid[0] if s == 1 else sb([P, S], F32, "hid%d" % s))
+            acc = bank(HALVES + h)
+            nc.tensor.matmul_mx(
+                acc[:], lhsT=w1_c[b][:, t * P : (t + 1) * P].bitcast(FP8X4), lhsT_scale=w1_s[b][:, t * P : (t + 1) * P],
+                rhs=v_c[:, half(h)].bitcast(FP8X4), rhs_scale=v_s[:, half(h)], start=True, stop=True,
+            )
+            nc.vector.tensor_tensor(hid[s][:, half(h)], acc[:], damp[s][:, half(h)], ALU.mult)
+
+        def renew(s, cols, entries):
+            nc.vector.tensor_tensor(pages[s][:].indirect(put[:, entries]), hid[s][:, cols], wg(SLICES[s][1])[:, cols], ALU.mult)
+
+        first, diff, moves = {}, {}, {}
+
+        def fetch_first(s):
+            first[s] = damp[s - 2][:, half(0)]
+            nc.vector.tensor_copy(first[s], pages[s][:].indirect(upper[:]))
+
+        def fetch_diff(s):
+            diff[s] = sb([P, PAIRS], F32, "diff", bufs=2)
+            nc.vector.tensor_tensor(diff[s][:], pages[s][:].indirect(lower[:]), first[s], ALU.subtract)
+
+        def compare(s):
+            b, t = SLICES[s]
+            moves[s] = rise, drop = damp[s][:, half(0)], damp[s - 2][:, half(1)]
+            nc.scalar.activation(rise, diff[s][:], ACT.Relu)
+            nc.scalar.activation(drop, diff[s][:], ACT.Relu, scale=-1.0)
+            nc.scalar.activation(drop, drop, ACT.Identity, scale=-1.0, bias=lift_t[:, b, t : t + 1])
+
+        def put_back(s, side):
+            nc.vector.tensor_tensor(pages[s][:].indirect((upper, lower)[side][:]), first[s], moves[s][side], ALU.add)
+
+        woven = {}
+
+        def weave(s, c, copy):
+            b, t = SLICES[s]
+            if (b, c) not in woven:
+                woven[b, c] = sb([P, BANK, PACK], BF16, "woven%d_%d" % (b, c))
+            copy(woven[b, c][:, :, t], pages[s][:, c * BANK : (c + 1) * BANK])
+
+        page_c, page_s = {}, {}
+
+        def quantise_page(b, c, codes):
+            page_c[b, c] = codes
+            page_s[b, c] = sb([P, BANK], U8, "page_s%d_%d" % (b, c))
+            nc.vector.quantize_mx(codes.bitcast(FP8X4), page_s[b, c][:], woven[b, c][:].rearrange("p c t -> p (c t)"))
+
+        sums = {}
+        BANK_OF = [4, 5, 6, 7, 0, 1, 2, 3]
+
+        def product(g, b):
+            c, nb = divmod(g, NB)
+            if b == 0:
+                sums[g] = bank(BANK_OF[g % BANKS])
+            nc.tensor.matmul_mx(
+                sums[g][:], lhsT=w4_c[b][:, nb * P : (nb + 1) * P].bitcast(FP8X4), lhsT_scale=w4_s[b][:, nb * P : (nb + 1) * P],
+                rhs=page_c[b, c].bitcast(FP8X4), rhs_scale=page_s[b, c][:], start=(b == 0), stop=(b == PASSES - 1),
+            )
+
+        log_spread([0], both_halves)
+        invert([0], both_halves)
+        quantise_w1(0, nc.vector.tensor_copy)
+        deal_w2_scales(1)
+        log_spread([1], both_halves)
+        invert([1], both_halves)
+        w4_raw = {0: load_w4(0)}
+        last = len(SLICES) - 1
+        for h in range(HALVES):
+            damped_bid(0, h)
+        for s in range(len(SLICES)):
+            if s == 0:
+                for h in range(HALVES):
+                    renew(s, half(h), half_list(h))
+            else:
+                renew(s, slice(0, S), slice(0, S // 16))
+            if s > 1:
+                put_back(s - 2, 0)
+            fetch_first(s)
+            if s > 1:
+                put_back(s - 2, 1)
+            fetch_diff(s)
+            compare(s)
+            if s < last:
+                for h in range(HALVES):
+                    damped_bid(s + 1, h)
+            if s == 0:
+                log_spread([2, 3, 4], whole)
+                invert([2, 3, 4], whole)
+                quantise_w1(1, nc.scalar.copy)
+                w4_raw[1] = load_w4(1)
+            if s > 1:
+                for c in range(CHUNKS):
+                    weave(s - 2, c, nc.scalar.copy)
+                if s + 3 <= last:
+                    load_page(s + 3)
+            if s == 1:
+                log_spread([5, 6, 7], whole)
+            if s == 2:
+                invert([5, 6, 7], whole)
+                quantise_w4(0, w4_raw[0])
+            if s == 3:
+                quantise_w4(1, w4_raw[1])
+            if s == 6:
+                codes0 = sb([P, T2], U32, "codes0")
+                for c in range(CHUNKS):
+                    quantise_page(0, c, codes0[:, c * BANK : (c + 1) * BANK])
+        for g in range(BANKS):
+            product(g, 0)
+        for s in (last - 1, last):
+            put_back(s, 0)
+            put_back(s, 1)
+            if s < last:
+                for c in range(CHUNKS):
+                    weave(s, c, nc.scalar.copy)
+
+        stage = [sb([P, 4, BANK], F32, "raw0"), sb([P, 4, BANK], F32, "raw1")]
+        stage2 = [sb([P, 2, BANK], F32, "hid0"), sb([P, 2, BANK], F32, "hid2")]
+
+        def staged(g):
+            return stage[g // 4][:, g % 4, :] if g < 8 else stage2[(g - 8) // 2][:, g % 2, :]
+
+        weave(last, 2, nc.scalar.copy)
+        for c in range(CHUNKS):
+            if c != 2:
+                weave(last, c, nc.vector.tensor_copy)
+            codes = sb([P, BANK], U32, "woven0_%d" % c)
+            quantise_page(1, c, codes[:])
+        for g in range(CHUNKS * NB):
+            c, nb = divmod(g, NB)
+            if g >= BANKS:
+                product(g, 0)
+            product(g, 1)
+            if g in (7, 9, 11):
+                nc.vector.tensor_scalar(staged(g), sums[g][:], gain_t[:, nb : nb + 1], None, ALU.mult)
+            else:
+                nc.scalar.activation(staged(g), sums[g][:], ACT.Copy, scale=gain_t[:, nb : nb + 1])
+            nc.sync.dma_start(out_rows[nb, :, c * BANK : (c + 1) * BANK], staged(g))

@@ -22,8 +22,10 @@ BANK = 512
 PASSES = H // (P * PACK)
 CHUNKS = T2 // BANK
 NB = N // P
-SLICES = [(0, 0), (0, 1), (0, 2), (0, 3), (1, 2), (1, 0), (1, 1), (1, 3)]
+SLICES = [(0, 0), (0, 1), (0, 2), (1, 2), (0, 3), (1, 0), (1, 1), (1, 3)]
+FLOAT_MAX = 3.4028234663852886e38
 BANKS = 8
+BID_BUFS = 2
 
 
 def tile_list_bill_demand_sheet_kernel(
@@ -86,12 +88,22 @@ def tile_list_bill_demand_sheet_kernel(
             nc.sync.dma_start(pages[s][:], page_rows[b, t])
 
         w1_raw = {0: load_w1(0)}
+        wg_tiles = {}
+
+        def load_wg(t0, t1):
+            rows = sb([P, t1 - t0, S], F32, "wg%d" % t0)
+            for q in range(4):
+                nc.sync.dma_start(rows[32 * q : 32 * q + 32, :, :], wgs_rows[:, t0:t1, :])
+            for t in range(t0, t1):
+                wg_tiles[t] = rows[:, t - t0, :]
+
+        load_wg(0, 1)
+        w1_raw[1] = load_w1(1)
         load_page(0)
         put = sb([P, S // 16], U16, "put")
         nc.sync.dma_start(put[:], offs2)
-        wg_first = sb([P, S], F32, "wg_first")
-        for q in range(4):
-            nc.sync.dma_start(wg_first[32 * q : 32 * q + 32, :], wgs_rows[:, 0, :])
+        load_wg(1, 2)
+        load_page(1)
         upper = sb([P, PAIRS // 16], U16, "upper")
         nc.sync.dma_start(upper[:], offs3)
         lower = sb([P, PAIRS // 16], U16, "lower")
@@ -101,29 +113,26 @@ def tile_list_bill_demand_sheet_kernel(
         with nc.allow_non_contiguous_dma(reason="one value a row"):
             nc.sync.dma_start(lift_t[:], lift.rearrange("(b p t) -> p b t", b=PASSES, t=PACK))
             nc.sync.dma_start(gain_t[:], gain.rearrange("(nb p) -> p nb", p=P))
-        wg_rest = sb([P, PACK - 1, S], F32, "wg_rest")
-        for q in range(4):
-            nc.sync.dma_start(wg_rest[32 * q : 32 * q + 32, :, :], wgs_rows[:, 1:PACK, :])
-        load_page(1)
-        w1_raw[1] = load_w1(1)
+        load_wg(2, PACK)
         load_page(2)
         load_page(3)
         load_page(4)
 
         def wg(t):
-            return wg_first[:] if t == 0 else wg_rest[:, t - 1, :]
+            return wg_tiles[t]
 
         w2_c = sb([P, 2 * H], U8, "w2_c")
-        w2_s = sb([P, H], U8, "w2_s")
+        w2_s = {}
         nc.vector.tensor_copy(
             w2_c[:].bitcast(U16).rearrange("p (b t m) -> p b t m", b=PASSES, t=PACK),
             w2_raw[:].bitcast(U16).rearrange("p (b m t) -> p b t m", b=PASSES, t=PACK),
         )
 
-        def deal_w2_scales(b):
+        def deal_w2_scales(b, tag):
             cols = slice(b * BANK, (b + 1) * BANK)
+            w2_s[b] = sb([P, BANK], U8, tag)
             nc.vector.tensor_copy(
-                w2_s[:, cols].rearrange("p (t m) -> p t m", t=PACK),
+                w2_s[b][:].rearrange("p (t m) -> p t m", t=PACK),
                 w2s_raw[:, cols].rearrange("p (m t) -> p t m", t=PACK),
             )
 
@@ -139,7 +148,7 @@ def tile_list_bill_demand_sheet_kernel(
 
         for h in range(HALVES):
             nc.vector.tensor_copy(v_s[:, half(h)], tab_s[:].indirect(pick[:, half_list(h)]))
-        deal_w2_scales(0)
+        deal_w2_scales(0, "w2_s0")
         for h in range(HALVES):
             nc.vector.tensor_copy(v_c[:, half(h)], tab_w[:].indirect(pick[:, half_list(h)]))
 
@@ -156,14 +165,15 @@ def tile_list_bill_demand_sheet_kernel(
             nc.vector.quantize_mx(w1_c[b][:].bitcast(FP8X4), w1_s[b][:], grouped[:])
 
         def quantise_w4(b, raw):
-            grouped = sb([P, PACK * N], BF16, "grouped%d" % b)
+            grouped = sb([P, PACK * N], BF16, ("grouped_w4", "grouped1")[b])
             nc.scalar.copy(grouped[:].rearrange("p (n j) -> p n j", j=PACK), raw[:].rearrange("p j n -> p n j"))
             w4_c[b] = sb([P, N], U32, "w4_c%d" % b)
             w4_s[b] = sb([P, N], U8, "w4_s%d" % b)
             nc.vector.quantize_mx(w4_c[b][:].bitcast(FP8X4), w4_s[b][:], grouped[:])
 
-        damp = {-2: sb([P, S], F32, "pair0"), -1: sb([P, S], F32, "pair1")}
-        SPREAD_BANKS = [0, 1, 4, 5, 6, 7]
+        damp = {}
+        SPREAD_BANK = [0, 4, 6, 0, 4, 6, 0, 4]
+        BID_BANK = [6, 0, 2, 2, 2, 2, 2, 2]
         both_halves = [half(h) for h in range(HALVES)]
         whole = [slice(0, S)]
 
@@ -173,9 +183,9 @@ def tile_list_bill_demand_sheet_kernel(
                 c0 = (b * PACK + t) * P
                 damp[s] = sb([P, S], F32, "damp%d" % s)
                 for h in range(HALVES):
-                    acc = bank(SPREAD_BANKS[(HALVES * s + h) % len(SPREAD_BANKS)])
+                    acc = bank(SPREAD_BANK[s] + h)
                     nc.tensor.matmul_mx(
-                        acc[:], lhsT=w2_c[:, 2 * c0 : 2 * (c0 + P)].bitcast(FP4X4), lhsT_scale=w2_s[:, c0 : c0 + P],
+                        acc[:], lhsT=w2_c[:, 2 * c0 : 2 * (c0 + P)].bitcast(FP4X4), lhsT_scale=w2_s[b][:, t * P : (t + 1) * P],
                         rhs=v_c[:, half(h)].bitcast(FP8X4), rhs_scale=v_s[:, half(h)], start=True, stop=True,
                     )
                     nc.scalar.activation(damp[s][:, half(h)], acc[:], ACT.Abs)
@@ -188,41 +198,62 @@ def tile_list_bill_demand_sheet_kernel(
                 for c in cuts:
                     nc.scalar.activation(damp[s][:, c], damp[s][:, c], ACT.Exp, scale=-1.0)
 
-        hid = {}
+        weighted = {}
 
-        def damped_bid(s, h):
+        def bid(s, h):
             b, t = SLICES[s]
-            if h == 0:
-                hid[s] = damp[s - 5] if s >= 3 else (hid[0] if s == 1 else sb([P, S], F32, "hid%d" % s))
-            acc = bank(HALVES + h)
+            acc = bank(BID_BANK[s] + h)
             nc.tensor.matmul_mx(
                 acc[:], lhsT=w1_c[b][:, t * P : (t + 1) * P].bitcast(FP8X4), lhsT_scale=w1_s[b][:, t * P : (t + 1) * P],
                 rhs=v_c[:, half(h)].bitcast(FP8X4), rhs_scale=v_s[:, half(h)], start=True, stop=True,
             )
-            nc.vector.tensor_tensor(hid[s][:, half(h)], acc[:], damp[s][:, half(h)], ALU.mult)
+            return acc
+
+        def weigh_from_psum(s):
+            weighted[s] = sb([P, S], F32, "weighted%d" % s)
+            for h in range(HALVES):
+                nc.vector.tensor_tensor(weighted[s][:, half(h)], bid(s, h)[:], wg(SLICES[s][1])[:, half(h)], ALU.mult)
+
+        bid_sb = {}
+
+        def stage_bid(s):
+            bid_sb[s] = sb([P, S], F32, "bid_sb", bufs=BID_BUFS)
+            for h in range(HALVES):
+                nc.scalar.copy(bid_sb[s][:, half(h)], bid(s, h)[:])
+
+        def weigh(s):
+            weighted[s] = damp[s - 1]
+            nc.gpsimd.tensor_tensor(weighted[s][:], bid_sb[s][:], wg(SLICES[s][1]), ALU.mult)
+
+        hid = {}
+
+        def dampen(s, cols, engine):
+            hid[s] = weighted[0] if s == 1 else weighted[s]
+            engine.tensor_tensor(hid[s][:, cols], weighted[s][:, cols], damp[s][:, cols], ALU.mult)
 
         def renew(s, cols, entries):
-            nc.vector.tensor_tensor(pages[s][:].indirect(put[:, entries]), hid[s][:, cols], wg(SLICES[s][1])[:, cols], ALU.mult)
+            nc.vector.tensor_copy(pages[s][:].indirect(put[:, entries]), hid[s][:, cols])
 
-        first, diff, moves = {}, {}, {}
+        pair_tiles = [sb([P, 2, PAIRS], F32, "pair"), sb([P, 2, PAIRS], F32, "pair_last")]
+        pair = {s: pair_tiles[s // (len(SLICES) - 1)] for s in range(len(SLICES))}
 
-        def fetch_first(s):
-            first[s] = damp[s - 2][:, half(0)]
-            nc.vector.tensor_copy(first[s], pages[s][:].indirect(upper[:]))
-
-        def fetch_diff(s):
-            diff[s] = sb([P, PAIRS], F32, "diff", bufs=2)
-            nc.vector.tensor_tensor(diff[s][:], pages[s][:].indirect(lower[:]), first[s], ALU.subtract)
+        def fetch(s):
+            nc.vector.tensor_copy(pair[s][:, 0, :], pages[s][:].indirect(upper[:]))
+            nc.vector.tensor_copy(pair[s][:, 1, :], pages[s][:].indirect(lower[:]))
 
         def compare(s):
             b, t = SLICES[s]
-            moves[s] = rise, drop = damp[s][:, half(0)], damp[s - 2][:, half(1)]
-            nc.scalar.activation(rise, diff[s][:], ACT.Relu)
-            nc.scalar.activation(drop, diff[s][:], ACT.Relu, scale=-1.0)
-            nc.scalar.activation(drop, drop, ACT.Identity, scale=-1.0, bias=lift_t[:, b, t : t + 1])
+            moves = damp[min(s + 1, len(SLICES) - 1)]
+            rise, drop = moves[:, half(0)], moves[:, half(1)]
+            first, second = pair[s][:, 0, :], pair[s][:, 1, :]
+            nc.gpsimd.tensor_tensor(drop, second, first, ALU.subtract)
+            nc.gpsimd.tensor_scalar(rise, drop, FLOAT_MAX, 0.0, ALU.min, ALU.max)
+            nc.gpsimd.tensor_tensor(first, first, rise, ALU.add)
+            nc.gpsimd.tensor_scalar(drop, rise, -1.0, lift_t[:, b, t : t + 1], ALU.mult, ALU.add)
+            nc.gpsimd.tensor_tensor(second, second, drop, ALU.add)
 
         def put_back(s, side):
-            nc.vector.tensor_tensor(pages[s][:].indirect((upper, lower)[side][:]), first[s], moves[s][side], ALU.add)
+            nc.vector.tensor_copy(pages[s][:].indirect((upper, lower)[side][:]), pair[s][:, side, :])
 
         woven = {}
 
@@ -251,64 +282,62 @@ def tile_list_bill_demand_sheet_kernel(
                 rhs=page_c[b, c].bitcast(FP8X4), rhs_scale=page_s[b, c][:], start=(b == 0), stop=(b == PASSES - 1),
             )
 
+        every, every_entry = slice(0, S), slice(0, S // 16)
+        last = len(SLICES) - 1
         log_spread([0], both_halves)
         invert([0], both_halves)
         quantise_w1(0, nc.vector.tensor_copy)
-        deal_w2_scales(1)
+        weigh_from_psum(0)
+        for h in range(HALVES):
+            dampen(0, half(h), nc.vector)
+        deal_w2_scales(1, "grouped0")
+        quantise_w1(1, nc.vector.tensor_copy)
+        weigh_from_psum(1)
         log_spread([1], both_halves)
         invert([1], both_halves)
-        w4_raw = {0: load_w4(0)}
-        last = len(SLICES) - 1
+        w4_raw = {b: load_w4(b) for b in range(PASSES)}
         for h in range(HALVES):
-            damped_bid(0, h)
+            renew(0, half(h), half_list(h))
+        dampen(1, every, nc.gpsimd)
+        stage_bid(2)
+        BATCHES = {0: [2, 3], 1: [4, 5], 2: [6, 7]}
         for s in range(len(SLICES)):
-            if s == 0:
-                for h in range(HALVES):
-                    renew(s, half(h), half_list(h))
-            else:
-                renew(s, slice(0, S), slice(0, S // 16))
-            if s > 1:
-                put_back(s - 2, 0)
-            fetch_first(s)
-            if s > 1:
-                put_back(s - 2, 1)
-            fetch_diff(s)
+            fetch(s)
+            if s == last:
+                put_back(s - 1, 0)
+                put_back(s - 1, 1)
+                for c in range(CHUNKS):
+                    weave(s - 1, c, nc.scalar.copy)
             compare(s)
             if s < last:
-                for h in range(HALVES):
-                    damped_bid(s + 1, h)
-            if s == 0:
-                log_spread([2, 3, 4], whole)
-                invert([2, 3, 4], whole)
-                quantise_w1(1, nc.scalar.copy)
-                w4_raw[1] = load_w4(1)
-            if s > 1:
+                renew(s + 1, every, every_entry)
+            if s in BATCHES:
+                log_spread(BATCHES[s], whole)
+                invert(BATCHES[s], whole)
+            if s + 2 <= last:
+                weigh(s + 2)
+                dampen(s + 2, every, nc.gpsimd)
+            if s + 3 <= last:
+                stage_bid(s + 3)
+            if s == last:
+                codes0 = [sb([P, 2, BANK], U32, "pair"), sb([P, 2, BANK], U32, "damp7")]
                 for c in range(CHUNKS):
-                    weave(s - 2, c, nc.scalar.copy)
-                if s + 3 <= last:
-                    load_page(s + 3)
-            if s == 1:
-                log_spread([5, 6, 7], whole)
-            if s == 2:
-                invert([5, 6, 7], whole)
-                quantise_w4(0, w4_raw[0])
-            if s == 3:
-                quantise_w4(1, w4_raw[1])
-            if s == 6:
-                codes0 = sb([P, T2], U32, "codes0")
+                    quantise_page(0, c, codes0[c // 2][:, c % 2, :])
+                for g in range(BANKS):
+                    product(g, 0)
+            if s != last - 1:
+                put_back(s, 0)
+                put_back(s, 1)
+            if 0 < s < last:
                 for c in range(CHUNKS):
-                    quantise_page(0, c, codes0[:, c * BANK : (c + 1) * BANK])
-        for g in range(BANKS):
-            product(g, 0)
-        for s in (last - 1, last):
-            put_back(s, 0)
-            put_back(s, 1)
-            if s < last:
-                for c in range(CHUNKS):
-                    weave(s, c, nc.scalar.copy)
+                    weave(s - 1, c, nc.scalar.copy)
+                if s + 4 <= last:
+                    load_page(s + 4)
+            if s in (4, 5):
+                quantise_w4(s - 4, w4_raw[s - 4])
 
         stage = [sb([P, 4, BANK], F32, "raw0"), sb([P, 4, BANK], F32, "raw1")]
-        stage2 = [sb([P, 2, BANK], F32, "hid0"), sb([P, 2, BANK], F32, "hid2")]
+        stage2 = [sb([P, 2, BANK], F32, "weighted0"), sb([P, 2, BANK], F32, "weighted1")]
 
         def staged(g):
             return stage[g // 4][:, g % 4, :] if g < 8 else stage2[(g - 8) // 2][:, g % 2, :]

@@ -22,10 +22,11 @@ BANK = 512
 PASSES = H // (P * PACK)
 CHUNKS = T2 // BANK
 NB = N // P
-SLICES = [(0, 0), (0, 1), (0, 2), (1, 2), (0, 3), (1, 0), (1, 1), (1, 3)]
+SLICES = [(0, 0), (0, 1), (0, 2), (0, 3), (1, 2), (1, 0), (1, 1), (1, 3)]
 FLOAT_MAX = 3.4028234663852886e38
 BANKS = 8
 BID_BUFS = 2
+PAGE_BUFS = 5
 
 
 def tile_list_bill_demand_sheet_kernel(
@@ -84,7 +85,7 @@ def tile_list_bill_demand_sheet_kernel(
 
         def load_page(s):
             b, t = SLICES[s]
-            pages[s] = sb([P, T2], F32, "page", bufs=5)
+            pages[s] = sb([P, T2], F32, "page", bufs=PAGE_BUFS)
             nc.sync.dma_start(pages[s][:], page_rows[b, t])
 
         w1_raw = {0: load_w1(0)}
@@ -97,23 +98,23 @@ def tile_list_bill_demand_sheet_kernel(
             for t in range(t0, t1):
                 wg_tiles[t] = rows[:, t - t0, :]
 
-        load_wg(0, 1)
-        w1_raw[1] = load_w1(1)
         load_page(0)
+        load_wg(0, 1)
         put = sb([P, S // 16], U16, "put")
         nc.sync.dma_start(put[:], offs2)
-        load_wg(1, 2)
-        load_page(1)
         upper = sb([P, PAIRS // 16], U16, "upper")
         nc.sync.dma_start(upper[:], offs3)
         lower = sb([P, PAIRS // 16], U16, "lower")
         nc.sync.dma_start(lower[:], offs4)
+        load_wg(1, 2)
         lift_t = sb([P, PASSES, PACK], F32, "lift_t")
         gain_t = sb([P, NB], F32, "gain_t")
         with nc.allow_non_contiguous_dma(reason="one value a row"):
             nc.sync.dma_start(lift_t[:], lift.rearrange("(b p t) -> p b t", b=PASSES, t=PACK))
+            load_page(1)
+            load_wg(2, PACK)
+            w1_raw[1] = load_w1(1)
             nc.sync.dma_start(gain_t[:], gain.rearrange("(nb p) -> p nb", p=P))
-        load_wg(2, PACK)
         load_page(2)
         load_page(3)
         load_page(4)
@@ -164,12 +165,10 @@ def tile_list_bill_demand_sheet_kernel(
             w1_s[b] = sb([P, BANK], U8, "w1_s%d" % b)
             nc.vector.quantize_mx(w1_c[b][:].bitcast(FP8X4), w1_s[b][:], grouped[:])
 
-        def quantise_w4(b, raw):
-            grouped = sb([P, PACK * N], BF16, ("grouped_w4", "grouped1")[b])
-            nc.scalar.copy(grouped[:].rearrange("p (n j) -> p n j", j=PACK), raw[:].rearrange("p j n -> p n j"))
-            w4_c[b] = sb([P, N], U32, "w4_c%d" % b)
+        def quantise_w4(b, grouped, codes):
+            w4_c[b] = codes
             w4_s[b] = sb([P, N], U8, "w4_s%d" % b)
-            nc.vector.quantize_mx(w4_c[b][:].bitcast(FP8X4), w4_s[b][:], grouped[:])
+            nc.vector.quantize_mx(codes.bitcast(FP8X4), w4_s[b][:], grouped)
 
         damp = {}
         SPREAD_BANK = [0, 4, 6, 0, 4, 6, 0, 4]
@@ -217,12 +216,12 @@ def tile_list_bill_demand_sheet_kernel(
         bid_sb = {}
 
         def stage_bid(s):
-            bid_sb[s] = sb([P, S], F32, "bid_sb", bufs=BID_BUFS)
+            bid_sb[s] = sb([P, S], F32, "grouped1") if s == 2 else sb([P, S], F32, "bid_sb", bufs=BID_BUFS)
             for h in range(HALVES):
                 nc.scalar.copy(bid_sb[s][:, half(h)], bid(s, h)[:])
 
         def weigh(s):
-            weighted[s] = damp[s - 1]
+            weighted[s] = damp[s - 1] if s > 1 else bid_sb[s]
             nc.gpsimd.tensor_tensor(weighted[s][:], bid_sb[s][:], wg(SLICES[s][1]), ALU.mult)
 
         hid = {}
@@ -234,8 +233,8 @@ def tile_list_bill_demand_sheet_kernel(
         def renew(s, cols, entries):
             nc.vector.tensor_copy(pages[s][:].indirect(put[:, entries]), hid[s][:, cols])
 
-        pair_tiles = [sb([P, 2, PAIRS], F32, "pair"), sb([P, 2, PAIRS], F32, "pair_last")]
-        pair = {s: pair_tiles[s // (len(SLICES) - 1)] for s in range(len(SLICES))}
+        pair_tiles = [sb([P, 2, PAIRS], F32, "pair0"), sb([P, 2, PAIRS], F32, "pair1")]
+        pair = {s: pair_tiles[s % 2] for s in range(len(SLICES))}
 
         def fetch(s):
             nc.vector.tensor_copy(pair[s][:, 0, :], pages[s][:].indirect(upper[:]))
@@ -243,14 +242,14 @@ def tile_list_bill_demand_sheet_kernel(
 
         def compare(s):
             b, t = SLICES[s]
-            moves = damp[min(s + 1, len(SLICES) - 1)]
+            moves = damp[1] if s == 0 else damp[min(s + 2, len(SLICES) - 1)]
             rise, drop = moves[:, half(0)], moves[:, half(1)]
             first, second = pair[s][:, 0, :], pair[s][:, 1, :]
             nc.gpsimd.tensor_tensor(drop, second, first, ALU.subtract)
             nc.gpsimd.tensor_scalar(rise, drop, FLOAT_MAX, 0.0, ALU.min, ALU.max)
-            nc.gpsimd.tensor_tensor(first, first, rise, ALU.add)
             nc.gpsimd.tensor_scalar(drop, rise, -1.0, lift_t[:, b, t : t + 1], ALU.mult, ALU.add)
-            nc.gpsimd.tensor_tensor(second, second, drop, ALU.add)
+            both = pair[s][:].rearrange("p side m -> p (side m)")
+            nc.gpsimd.tensor_tensor(both, both, moves[:], ALU.add)
 
         def put_back(s, side):
             nc.vector.tensor_copy(pages[s][:].indirect((upper, lower)[side][:]), pair[s][:, side, :])
@@ -271,16 +270,21 @@ def tile_list_bill_demand_sheet_kernel(
             nc.vector.quantize_mx(codes.bitcast(FP8X4), page_s[b, c][:], woven[b, c][:].rearrange("p c t -> p (c t)"))
 
         sums = {}
-        BANK_OF = [4, 5, 6, 7, 0, 1, 2, 3]
+        GROUPS = CHUNKS * NB
+        PARKED = range(BANKS, GROUPS)
 
         def product(g, b):
             c, nb = divmod(g, NB)
-            if b == 0:
-                sums[g] = bank(BANK_OF[g % BANKS])
+            if b == 0 or g in PARKED:
+                sums[g] = bank(g % BANKS)
             nc.tensor.matmul_mx(
                 sums[g][:], lhsT=w4_c[b][:, nb * P : (nb + 1) * P].bitcast(FP8X4), lhsT_scale=w4_s[b][:, nb * P : (nb + 1) * P],
-                rhs=page_c[b, c].bitcast(FP8X4), rhs_scale=page_s[b, c][:], start=(b == 0), stop=(b == PASSES - 1),
+                rhs=page_c[b, c].bitcast(FP8X4), rhs_scale=page_s[b, c][:],
+                start=(b == 0 or g in PARKED), stop=(b == PASSES - 1 or g in PARKED),
             )
+
+        def scaled_out(g, rows):
+            nc.scalar.activation(rows, sums[g][:], ACT.Copy, scale=gain_t[:, g % NB : g % NB + 1])
 
         every, every_entry = slice(0, S), slice(0, S // 16)
         last = len(SLICES) - 1
@@ -291,24 +295,31 @@ def tile_list_bill_demand_sheet_kernel(
         for h in range(HALVES):
             dampen(0, half(h), nc.vector)
         deal_w2_scales(1, "grouped0")
-        quantise_w1(1, nc.vector.tensor_copy)
-        weigh_from_psum(1)
+        stage_bid(1)
+        weigh(1)
         log_spread([1], both_halves)
         invert([1], both_halves)
         w4_raw = {b: load_w4(b) for b in range(PASSES)}
         for h in range(HALVES):
             renew(0, half(h), half_list(h))
-        dampen(1, every, nc.gpsimd)
+        for h in range(HALVES):
+            dampen(1, half(h), nc.gpsimd)
         stage_bid(2)
         BATCHES = {0: [2, 3], 1: [4, 5], 2: [6, 7]}
+
+        def exchange(s):
+            put_back(s, 0)
+            put_back(s, 1)
+            if s < last - 1:
+                for c in range(CHUNKS):
+                    weave(s, c, nc.scalar.copy)
+            if s + PAGE_BUFS <= last:
+                load_page(s + PAGE_BUFS)
+
         for s in range(len(SLICES)):
             fetch(s)
-            if s == last:
-                put_back(s - 1, 0)
-                put_back(s - 1, 1)
-                for c in range(CHUNKS):
-                    weave(s - 1, c, nc.scalar.copy)
-            compare(s)
+            if s == 0:
+                compare(s)
             if s < last:
                 renew(s + 1, every, every_entry)
             if s in BATCHES:
@@ -317,44 +328,50 @@ def tile_list_bill_demand_sheet_kernel(
             if s + 2 <= last:
                 weigh(s + 2)
                 dampen(s + 2, every, nc.gpsimd)
+            if s == 0:
+                quantise_w1(1, lambda rounded, raw: nc.gpsimd.tensor_scalar(rounded, raw, 1.0, 0.0, ALU.mult, ALU.add))
             if s + 3 <= last:
                 stage_bid(s + 3)
-            if s == last:
-                codes0 = [sb([P, 2, BANK], U32, "pair"), sb([P, 2, BANK], U32, "damp7")]
-                for c in range(CHUNKS):
-                    quantise_page(0, c, codes0[c // 2][:, c % 2, :])
-                for g in range(BANKS):
-                    product(g, 0)
-            if s != last - 1:
-                put_back(s, 0)
-                put_back(s, 1)
-            if 0 < s < last:
-                for c in range(CHUNKS):
-                    weave(s - 1, c, nc.scalar.copy)
-                if s + 4 <= last:
-                    load_page(s + 4)
-            if s in (4, 5):
-                quantise_w4(s - 4, w4_raw[s - 4])
+            if s != 1:
+                exchange(max(s - 1, 0))
+            if s > 0:
+                compare(s)
+            if s == last - 1:
+                grouped = sb([P, PASSES, PACK * N], BF16, "damp6")
+                for b in range(PASSES):
+                    nc.scalar.copy(grouped[:, b, :].rearrange("p (n j) -> p n j", j=PACK), w4_raw[b][:].rearrange("p j n -> p n j"))
+        codes0 = [sb([P, 2 * BANK + PASSES * N], U32, "pair0"), sb([P, 2 * BANK], U32, "damp7")]
+        for b in range(PASSES):
+            quantise_w4(b, grouped[:, b, :], codes0[0][:, 2 * BANK + b * N : 2 * BANK + (b + 1) * N])
+        for i, c in enumerate((2, 3, 0, 1)):
+            quantise_page(0, c, codes0[i // 2][:, half(i % 2)])
+        parked = sb([P, len(PARKED), BANK], F32, "wg2")
+        for g in PARKED:
+            product(g, 0)
+            scaled_out(g, parked[:, g - BANKS, :])
+        for g in range(BANKS):
+            product(g, 0)
+        for c in range(CHUNKS):
+            weave(last - 1, c, nc.scalar.copy)
+        exchange(last)
 
         stage = [sb([P, 4, BANK], F32, "raw0"), sb([P, 4, BANK], F32, "raw1")]
-        stage2 = [sb([P, 2, BANK], F32, "weighted0"), sb([P, 2, BANK], F32, "weighted1")]
+        stage2 = [sb([P, 2, BANK], F32, "weighted0"), sb([P, 2, BANK], F32, "damp0")]
 
         def staged(g):
             return stage[g // 4][:, g % 4, :] if g < 8 else stage2[(g - 8) // 2][:, g % 2, :]
 
-        weave(last, 2, nc.scalar.copy)
         for c in range(CHUNKS):
-            if c != 2:
-                weave(last, c, nc.vector.tensor_copy)
+            weave(last, c, nc.vector.tensor_copy)
             codes = sb([P, BANK], U32, "woven0_%d" % c)
             quantise_page(1, c, codes[:])
-        for g in range(CHUNKS * NB):
+        for g in range(GROUPS):
             c, nb = divmod(g, NB)
-            if g >= BANKS:
-                product(g, 0)
             product(g, 1)
-            if g in (7, 9, 11):
-                nc.vector.tensor_scalar(staged(g), sums[g][:], gain_t[:, nb : nb + 1], None, ALU.mult)
+            if g in PARKED:
+                nc.vector.scalar_tensor_tensor(
+                    staged(g), sums[g][:], gain_t[:, nb : nb + 1], parked[:, g - BANKS, :], ALU.mult, ALU.add
+                )
             else:
-                nc.scalar.activation(staged(g), sums[g][:], ACT.Copy, scale=gain_t[:, nb : nb + 1])
+                scaled_out(g, staged(g))
             nc.sync.dma_start(out_rows[nb, :, c * BANK : (c + 1) * BANK], staged(g))

from contextlib import ExitStack

import concourse.mybir as mybir

K, H, N, T, S, T2, PAIRS = 512, 1024, 384, 4096, 1024, 2048, 512
FLOPS = 2 * (2 * K * H * S + H * N * T2)

F32 = mybir.dt.float32
BF16 = mybir.dt.bfloat16
I32 = mybir.dt.int32
U32 = mybir.dt.uint32
U16 = mybir.dt.uint16
U8 = mybir.dt.uint8
FP8X4 = mybir.dt.float8_e4m3fn_x4
FP4X4 = mybir.dt.float4_e2m1fn_x4
ACT = mybir.ActivationFunctionType
ALU = mybir.AluOpType

P = 128
PACK = 4
BANK = 512
PASSES = H // (P * PACK)
CHUNKS = T2 // BANK
NB = N // P
SLICES = [(0, 0), (0, 1), (0, 2), (0, 3), (1, 2), (1, 0), (1, 1), (1, 3)]
FLOAT_MAX = 3.4028234663852886e38
BANKS = 8
BID_BUFS = 2
PAGE_BUFS = 5


def tile_list_bill_demand_sheet_kernel(
    tc, tab_words, tab_scales, offs, offs2, offs3, offs4, w1, w2_words, w2_scales, wgs, page0, lift, w4, gain, out
):
    nc = tc.nc
    with ExitStack() as ctx:
        pool = ctx.enter_context(tc.tile_pool(name="sb", bufs=1))
        psum = ctx.enter_context(tc.psum_pool(name="ps", bufs=1))

        def sb(shape, dtype, tag, bufs=1):
            return pool.tile(shape, dtype, name=tag, tag=tag, bufs=bufs, align_bytes=64)

        def bank(i):
            return psum.tile([P, BANK], F32, name="bank%d" % i, tag="bank%d" % i)

        page_rows = page0.rearrange("(b p t) c -> b t p c", b=PASSES, t=PACK)
        w1_rows = w1.rearrange("(p j) (b c) -> b p j c", j=PACK, b=PASSES)
        w4_rows = w4.rearrange("(b p j) n -> b p j n", b=PASSES, j=PACK)
        wgs_rows = wgs.rearrange("(q t) j -> q t j", t=PACK)
        out_rows = out.rearrange("(nb p) c -> nb p c", p=P)

        pick = sb([P, S // 16], U16, "pick")
        nc.sync.dma_start(pick[:], offs)
        tab_s = sb([P, T], U8, "tab_s")
        nc.vector.memset(tab_s[:].bitcast(I32), 0)
        w2s_raw = sb([P, H], U8, "w2s_raw")
        nc.vector.memset(w2s_raw[:].bitcast(I32), 0)
        tab_w = sb([P, T], U32, "tab_w")
        tab_rows = tab_words[0].rearrange("p t i -> p (t i)").bitcast(I32)

        def load_plane(plane, rows, q):
            nc.sync.dma_start(plane[32 * q : 32 * q + 4, :].bitcast(I32), rows[0, 4 * q : 4 * q + 4, :].bitcast(I32))

        nc.sync.dma_start(tab_w[:, : T // 2].bitcast(I32), tab_rows[:, : T // 2])
        for q in range(4):
            load_plane(tab_s, tab_scales, q)
        w2_raw = sb([P, 2 * H], U8, "w2_raw")
        nc.sync.dma_start(w2_raw[:].bitcast(I32), w2_words[0].bitcast(I32))
        load_plane(w2s_raw, w2_scales, 0)
        nc.sync.dma_start(tab_w[:, T // 2 :].bitcast(I32), tab_rows[:, T // 2 :])
        for q in range(1, 4):
            load_plane(w2s_raw, w2_scales, q)

        def load_w1(b):
            raw = sb([P, PACK, BANK], F32, "raw%d" % b)
            nc.sync.dma_start(raw[:], w1_rows[b])
            return raw

        def load_w4(b):
            raw = sb([P, PACK, N], F32, "raw%d" % b)
            nc.sync.dma_start(raw[:], w4_rows[b])
            return raw

        pages = {}

        def load_page(s):
            b, t = SLICES[s]
            pages[s] = sb([P, T2], F32, "page", bufs=PAGE_BUFS)
            nc.sync.dma_start(pages[s][:], page_rows[b, t])

        w1_raw = {0: load_w1(0)}
        wg_tiles = {}

        def load_wg(t0, t1):
            rows = sb([P, t1 - t0, S], F32, "wg%d" % t0)
            for q in range(4):
                nc.sync.dma_start(rows[32 * q : 32 * q + 32, :, :], wgs_rows[:, t0:t1, :])
            for t in range(t0, t1):
                wg_tiles[t] = rows[:, t - t0, :]

        load_page(0)
        load_wg(0, 1)
        put = sb([P, S // 16], U16, "put")
        nc.sync.dma_start(put[:], offs2)
        upper = sb([P, PAIRS // 16], U16, "upper")
        nc.sync.dma_start(upper[:], offs3)
        lower = sb([P, PAIRS // 16], U16, "lower")
        nc.sync.dma_start(lower[:], offs4)
        load_wg(1, 2)
        lift_t = sb([P, PASSES, PACK], F32, "lift_t")
        gain_t = sb([P, NB], F32, "gain_t")
        with nc.allow_non_contiguous_dma(reason="one value a row"):
            nc.sync.dma_start(lift_t[:], lift.rearrange("(b p t) -> p b t", b=PASSES, t=PACK))
            load_page(1)
            load_wg(2, PACK)
            w1_raw[1] = load_w1(1)
            nc.sync.dma_start(gain_t[:], gain.rearrange("(nb p) -> p nb", p=P))
        load_page(2)
        load_page(3)
        load_page(4)

        def wg(t):
            return wg_tiles[t]

        w2_c = sb([P, 2 * H], U8, "w2_c")
        w2_s = {}
        nc.vector.tensor_copy(
            w2_c[:].bitcast(U16).rearrange("p (b t m) -> p b t m", b=PASSES, t=PACK),
            w2_raw[:].bitcast(U16).rearrange("p (b m t) -> p b t m", b=PASSES, t=PACK),
        )

        def deal_w2_scales(b, tag):
            cols = slice(b * BANK, (b + 1) * BANK)
            w2_s[b] = sb([P, BANK], U8, tag)
            nc.vector.tensor_copy(
                w2_s[b][:].rearrange("p (t m) -> p t m", t=PACK),
                w2s_raw[:, cols].rearrange("p (m t) -> p t m", t=PACK),
            )

        v_c = sb([P, S], U32, "v_c")
        v_s = sb([P, S], U8, "v_s")
        HALVES = S // BANK

        def half(h):
            return slice(h * BANK, (h + 1) * BANK)

        def half_list(h):
            return slice(h * BANK // 16, (h + 1) * BANK // 16)

        for h in range(HALVES):
            nc.vector.tensor_copy(v_s[:, half(h)], tab_s[:].indirect(pick[:, half_list(h)]))
        deal_w2_scales(0, "w2_s0")
        for h in range(HALVES):
            nc.vector.tensor_copy(v_c[:, half(h)], tab_w[:].indirect(pick[:, half_list(h)]))

        w1_c, w1_s, w4_c, w4_s = {}, {}, {}, {}

        def quantise_w1(b, copy):
            grouped = sb([P, PACK * BANK], BF16, "grouped%d" % b)
            copy(
                grouped[:].rearrange("p (t m j) -> p m t j", t=PACK, j=PACK),
                w1_raw[b][:].rearrange("p j (m t) -> p m t j", t=PACK),
            )
            w1_c[b] = sb([P, BANK], U32, "w1_c%d" % b)
            w1_s[b] = sb([P, BANK], U8, "w1_s%d" % b)
            nc.vector.quantize_mx(w1_c[b][:].bitcast(FP8X4), w1_s[b][:], grouped[:])

        def quantise_w4(b, grouped, codes):
            w4_c[b] = codes
            w4_s[b] = sb([P, N], U8, "w4_s%d" % b)
            nc.vector.quantize_mx(codes.bitcast(FP8X4), w4_s[b][:], grouped)

        damp = {}
        SPREAD_BANK = [0, 4, 6, 0, 4, 6, 0, 4]
        BID_BANK = [6, 0, 2, 2, 2, 2, 2, 2]
        both_halves = [half(h) for h in range(HALVES)]
        whole = [slice(0, S)]

        def log_spread(batch, cuts):
            for s in batch:
                b, t = SLICES[s]
                c0 = (b * PACK + t) * P
                damp[s] = sb([P, S], F32, "damp%d" % s)
                for h in range(HALVES):
                    acc = bank(SPREAD_BANK[s] + h)
                    nc.tensor.matmul_mx(
                        acc[:], lhsT=w2_c[:, 2 * c0 : 2 * (c0 + P)].bitcast(FP4X4), lhsT_scale=w2_s[b][:, t * P : (t + 1) * P],
                        rhs=v_c[:, half(h)].bitcast(FP8X4), rhs_scale=v_s[:, half(h)], start=True, stop=True,
                    )
                    nc.scalar.activation(damp[s][:, half(h)], acc[:], ACT.Abs)
            for s in batch:
                for c in cuts:
                    nc.scalar.activation(damp[s][:, c], damp[s][:, c], ACT.Ln, bias=1.0)

        def invert(batch, cuts):
            for s in batch:
                for c in cuts:
                    nc.scalar.activation(damp[s][:, c], damp[s][:, c], ACT.Exp, scale=-1.0)

        weighted = {}

        def bid(s, h):
            b, t = SLICES[s]
            acc = bank(BID_BANK[s] + h)
            nc.tensor.matmul_mx(
                acc[:], lhsT=w1_c[b][:, t * P : (t + 1) * P].bitcast(FP8X4), lhsT_scale=w1_s[b][:, t * P : (t + 1) * P],
                rhs=v_c[:, half(h)].bitcast(FP8X4), rhs_scale=v_s[:, half(h)], start=True, stop=True,
            )
            return acc

        def weigh_from_psum(s):
            weighted[s] = sb([P, S], F32, "weighted%d" % s)
            for h in range(HALVES):
                nc.vector.tensor_tensor(weighted[s][:, half(h)], bid(s, h)[:], wg(SLICES[s][1])[:, half(h)], ALU.mult)

        bid_sb = {}

        def stage_bid(s):
            bid_sb[s] = sb([P, S], F32, "grouped1") if s == 2 else sb([P, S], F32, "bid_sb", bufs=BID_BUFS)
            for h in range(HALVES):
                nc.scalar.copy(bid_sb[s][:, half(h)], bid(s, h)[:])

        def weigh(s):
            weighted[s] = damp[s - 1] if s > 1 else bid_sb[s]
            nc.gpsimd.tensor_tensor(weighted[s][:], bid_sb[s][:], wg(SLICES[s][1]), ALU.mult)

        hid = {}

        def dampen(s, cols, engine):
            hid[s] = weighted[0] if s == 1 else weighted[s]
            engine.tensor_tensor(hid[s][:, cols], weighted[s][:, cols], damp[s][:, cols], ALU.mult)

        def renew(s, cols, entries):
            nc.vector.tensor_copy(pages[s][:].indirect(put[:, entries]), hid[s][:, cols])

        pair_tiles = [sb([P, 2, PAIRS], F32, "pair0"), sb([P, 2, PAIRS], F32, "pair1")]
        pair = {s: pair_tiles[s % 2] for s in range(len(SLICES))}

        def fetch(s):
            nc.vector.tensor_copy(pair[s][:, 0, :], pages[s][:].indirect(upper[:]))
            nc.vector.tensor_copy(pair[s][:, 1, :], pages[s][:].indirect(lower[:]))

        def compare(s):
            b, t = SLICES[s]
            moves = damp[1] if s == 0 else damp[min(s + 2, len(SLICES) - 1)]
            rise, drop = moves[:, half(0)], moves[:, half(1)]
            first, second = pair[s][:, 0, :], pair[s][:, 1, :]
            nc.gpsimd.tensor_tensor(drop, second, first, ALU.subtract)
            nc.gpsimd.tensor_scalar(rise, drop, FLOAT_MAX, 0.0, ALU.min, ALU.max)
            nc.gpsimd.tensor_scalar(drop, rise, -1.0, lift_t[:, b, t : t + 1], ALU.mult, ALU.add)
            both = pair[s][:].rearrange("p side m -> p (side m)")
            nc.gpsimd.tensor_tensor(both, both, moves[:], ALU.add)

        def put_back(s, side):
            nc.vector.tensor_copy(pages[s][:].indirect((upper, lower)[side][:]), pair[s][:, side, :])

        woven = {}

        def weave(s, c, copy):
            b, t = SLICES[s]
            if (b, c) not in woven:
                woven[b, c] = sb([P, BANK, PACK], BF16, "woven%d_%d" % (b, c))
            copy(woven[b, c][:, :, t], pages[s][:, c * BANK : (c + 1) * BANK])

        page_c, page_s = {}, {}

        def quantise_page(b, c, codes):
            page_c[b, c] = codes
            page_s[b, c] = sb([P, BANK], U8, "page_s%d_%d" % (b, c))
            nc.vector.quantize_mx(codes.bitcast(FP8X4), page_s[b, c][:], woven[b, c][:].rearrange("p c t -> p (c t)"))

        sums = {}
        GROUPS = CHUNKS * NB
        PARKED = range(BANKS, GROUPS)

        def product(g, b):
            c, nb = divmod(g, NB)
            if b == 0 or g in PARKED:
                sums[g] = bank(g % BANKS)
            nc.tensor.matmul_mx(
                sums[g][:], lhsT=w4_c[b][:, nb * P : (nb + 1) * P].bitcast(FP8X4), lhsT_scale=w4_s[b][:, nb * P : (nb + 1) * P],
                rhs=page_c[b, c].bitcast(FP8X4), rhs_scale=page_s[b, c][:],
                start=(b == 0 or g in PARKED), stop=(b == PASSES - 1 or g in PARKED),
            )

        def scaled_out(g, rows):
            nc.scalar.activation(rows, sums[g][:], ACT.Copy, scale=gain_t[:, g % NB : g % NB + 1])

        every, every_entry = slice(0, S), slice(0, S // 16)
        last = len(SLICES) - 1
        log_spread([0], both_halves)
        invert([0], both_halves)
        quantise_w1(0, nc.vector.tensor_copy)
        weigh_from_psum(0)
        for h in range(HALVES):
            dampen(0, half(h), nc.vector)
        deal_w2_scales(1, "grouped0")
        stage_bid(1)
        weigh(1)
        log_spread([1], both_halves)
        invert([1], both_halves)
        w4_raw = {b: load_w4(b) for b in range(PASSES)}
        for h in range(HALVES):
            renew(0, half(h), half_list(h))
        for h in range(HALVES):
            dampen(1, half(h), nc.gpsimd)
        stage_bid(2)
        BATCHES = {0: [2, 3], 1: [4, 5], 2: [6, 7]}

        def exchange(s):
            put_back(s, 0)
            put_back(s, 1)
            if s < last - 1:
                for c in range(CHUNKS):
                    weave(s, c, nc.scalar.copy)
            if s + PAGE_BUFS <= last:
                load_page(s + PAGE_BUFS)

        for s in range(len(SLICES)):
            fetch(s)
            if s == 0:
                compare(s)
            if s < last:
                renew(s + 1, every, every_entry)
            if s in BATCHES:
                log_spread(BATCHES[s], whole)
                invert(BATCHES[s], whole)
            if s + 2 <= last:
                weigh(s + 2)
                dampen(s + 2, every, nc.gpsimd)
            if s == 0:
                quantise_w1(1, lambda rounded, raw: nc.gpsimd.tensor_scalar(rounded, raw, 1.0, 0.0, ALU.mult, ALU.add))
            if s + 3 <= last:
                stage_bid(s + 3)
            if s != 1:
                exchange(max(s - 1, 0))
            if s > 0:
                compare(s)
            if s == last - 1:
                grouped = sb([P, PASSES, PACK * N], BF16, "damp6")
                for b in range(PASSES):
                    nc.scalar.copy(grouped[:, b, :].rearrange("p (n j) -> p n j", j=PACK), w4_raw[b][:].rearrange("p j n -> p n j"))
        codes0 = [sb([P, 2 * BANK + PASSES * N], U32, "pair0"), sb([P, 2 * BANK], U32, "damp7")]
        for b in range(PASSES):
            quantise_w4(b, grouped[:, b, :], codes0[0][:, 2 * BANK + b * N : 2 * BANK + (b + 1) * N])
        for i, c in enumerate((2, 3, 0, 1)):
            quantise_page(0, c, codes0[i // 2][:, half(i % 2)])
        parked = sb([P, len(PARKED), BANK], F32, "wg2")
        for g in PARKED:
            product(g, 0)
            scaled_out(g, parked[:, g - BANKS, :])
        for g in range(BANKS):
            product(g, 0)
        for c in range(CHUNKS):
            weave(last - 1, c, nc.scalar.copy)
        exchange(last)

        stage = [sb([P, 4, BANK], F32, "raw0"), sb([P, 4, BANK], F32, "raw1")]
        stage2 = [sb([P, 2, BANK], F32, "weighted0"), sb([P, 2, BANK], F32, "damp0")]

        def staged(g):
            return stage[g // 4][:, g % 4, :] if g < 8 else stage2[(g - 8) // 2][:, g % 2, :]

        for c in range(CHUNKS):
            weave(last, c, nc.vector.tensor_copy)
            codes = sb([P, BANK], U32, "woven0_%d" % c)
            quantise_page(1, c, codes[:])
        for g in range(GROUPS):
            c, nb = divmod(g, NB)
            product(g, 1)
            if g in PARKED:
                nc.vector.scalar_tensor_tensor(
                    staged(g), sums[g][:], gain_t[:, nb : nb + 1], parked[:, g - BANKS, :], ALU.mult, ALU.add
                )
            else:
                scaled_out(g, staged(g))
            nc.sync.dma_start(out_rows[nb, :, c * BANK : (c + 1) * BANK], staged(g))
